import numpy as np
import ml_dtypes


def mxq(x, axis, fmt="e4m3"):
    dtype, down = {"e4m3": (ml_dtypes.float8_e4m3fn, 7), "e5m2": (ml_dtypes.float8_e5m2, 14)}[fmt]
    v = np.moveaxis(np.asarray(x, np.float32).astype(ml_dtypes.bfloat16).astype(np.float64), axis, -1)
    blocks = v.reshape(v.shape[:-1] + (-1, 32))
    amax = np.abs(blocks).max(-1, keepdims=True)
    byte = np.maximum(np.where(amax > 0, np.frexp(amax)[1] - 1 + 127, 0) - down, 1)
    scale = np.exp2(byte - 127.0)
    codes = (blocks / scale).astype(np.float32).astype(dtype).astype(np.float64)
    return np.moveaxis((codes * scale).reshape(v.shape), -1, axis)


WIDE = False


def mx_kscale(k):
    if not WIDE:
        return np.ones(k)
    levels = np.array([10, -10, 5, -5, 0])
    if k % 512:
        return np.exp2(np.random.permutation(np.resize(levels, k // 32))).repeat(32)
    a = np.empty((k // 512, 16))
    for p in range(k // 512):
        a[p, :8] = np.random.permutation(np.resize(levels, 8))
        for g in range(8):
            far = levels[np.abs(levels - a[p, g]) >= 10]
            a[p, g + 8] = far[np.random.randint(len(far))]
    return np.exp2(a.ravel()).repeat(32)


def f64(x):
    return np.asarray(x).astype(np.float64)


def striped8(idx):
    return np.asarray(idx).reshape(8, -1, 16).transpose(0, 2, 1).reshape(128, -1).astype(np.uint16)


def unstriped8(offs):
    return offs.reshape(8, 16, -1).transpose(0, 2, 1).reshape(8, -1).astype(np.int64)


def pick8(x, idx, run):
    r = np.arange(len(x))
    return x[r[:, None], idx[r % (8 * run) // run]]


E2M1 = np.array([0.0, 0.5, 1.0, 1.5, 2.0, 3.0, 4.0, 6.0, -0.0, -0.5, -1.0, -1.5, -2.0, -3.0, -4.0, -6.0])


def pack_weight(w, fmt):
    k, n = w.shape
    w = f64(np.asarray(w, np.float32).astype(ml_dtypes.bfloat16)).reshape(k // 32, 32, n)
    amax = np.abs(w).max(1)
    if fmt == "e4m3":
        byte = np.frexp(amax)[1] - 1 + 127 - 7
    else:
        mant, ex = np.frexp(amax / 6.0)
        byte = np.where(mant > 0.5, ex, ex - 1) + 127
    byte = np.clip(np.where(amax > 0, byte, 1), 1, 254)
    scaled = (w * np.exp2(127.0 - byte)[:, None, :]).reshape(k, n).astype(np.float32)
    by_word = np.ascontiguousarray(scaled.reshape(k // 512, 128, 4, n).transpose(0, 1, 3, 2))
    if fmt == "e4m3":
        words = by_word.astype(ml_dtypes.float8_e4m3fn).view(np.uint8)
    else:
        c = by_word.astype(ml_dtypes.float4_e2m1fn).view(np.uint8) & 0xF
        words = (c[..., 0::2] | (c[..., 1::2] << 4)).reshape(k // 512, 128, 2 * n)
    return np.ascontiguousarray(words), np.ascontiguousarray(byte.astype(np.uint8).reshape(k // 512, 16, n))


def unpack_weight(words, scales, fmt):
    g, _, n = scales.shape
    words = np.ascontiguousarray(words).reshape(g, 128, n, -1)
    if fmt == "e4m3":
        vals = words.view(ml_dtypes.float8_e4m3fn).astype(np.float64)
    else:
        nib = np.empty((g, 128, n, 4), np.uint8)
        nib[..., 0::2] = words & 0xF
        nib[..., 1::2] = words >> 4
        vals = E2M1[nib]
    vals = vals * np.repeat(np.exp2(scales.astype(np.float64) - 127.0), 8, axis=1)[..., None]
    return vals.transpose(0, 1, 3, 2).reshape(g * 512, n)


def sigmoid(v):
    return 1.0 / (1.0 + np.exp(-v))


D, T, U, X, I, Q = 512, 1024, 1024, 1024, 512, 128


def setup_inputs():
    n = np.random.standard_normal
    idx = np.stack([np.random.permutation(T)[:I] for _ in range(8)])
    idx2 = np.stack([np.random.permutation(U)[:I] for _ in range(8)])
    idx3 = np.stack([np.random.permutation(X)[:I] for _ in range(8)])
    idx4 = np.stack([np.random.permutation(X)[:I] for _ in range(8)])
    idx5 = np.stack([np.random.permutation(X)[:I] for _ in range(8)])
    fd = mx_kscale(D)
    keysp = pack_weight(n((D, T)) / fd[:, None], "e2m1")
    notesp = pack_weight(n((D, U)) / fd[:, None], "e4m3")
    usersp = pack_weight(n((D, X)) / fd[:, None], "e2m1")
    return {
        "query": (n((D, Q)) * 1.0 / np.sqrt(D) * fd[:, None]).astype(np.float32),
        "keys_words": keysp[0],
        "keys_scales": keysp[1],
        "notes_words": notesp[0],
        "notes_scales": notesp[1],
        "users_words": usersp[0],
        "users_scales": usersp[1],
        "thr": (np.random.uniform(-0.6, 0.6, (Q, 1))).astype(np.float32),
        "slope": (np.random.uniform(1.0, 3.0, (Q, 1))).astype(np.float32),
        "offs": striped8(idx),
        "offs2": striped8(idx2),
        "offs3": striped8(idx3),
        "offs4": striped8(idx4),
        "offs5": striped8(idx5),
    }


def reference(query, keys_words, keys_scales, notes_words, notes_scales, users_words, users_scales, thr, slope, offs, offs2, offs3, offs4, offs5):
    idx = unstriped8(offs)
    idx2 = unstriped8(offs2)
    idx3 = unstriped8(offs3)
    idx4 = unstriped8(offs4)
    idx5 = unstriped8(offs5)
    keysu = unpack_weight(keys_words, keys_scales, "e2m1")
    notesu = unpack_weight(notes_words, notes_scales, "e4m3")
    usersu = unpack_weight(users_words, users_scales, "e2m1")
    queryq = mxq(f64(query), 0, "e4m3")
    a = queryq.T @ keysu
    b = queryq.T @ notesu
    c0 = queryq.T @ usersu
    s1 = sigmoid(pick8(a, idx, 16) * f64(slope) + f64(thr))
    s2 = sigmoid(pick8(b, idx2, 16) * f64(slope) + f64(thr))
    w = pick8(c0, idx3, 16) * s1
    v = w - s2
    f1 = np.zeros((Q, X))
    f1[np.arange(Q)[:, None], idx4[np.arange(Q) % 128 // 16]] = v
    cc = c0 + f1
    y = pick8(cc, idx5, 16)
    return y

@@ -1,0 +1,159 @@
+from contextlib import ExitStack
+
+import concourse.mybir as mybir
+
+F32 = mybir.dt.float32
+BF16 = mybir.dt.bfloat16
+I32 = mybir.dt.int32
+U32 = mybir.dt.uint32
+U16 = mybir.dt.uint16
+U8 = mybir.dt.uint8
+FP8X4 = mybir.dt.float8_e4m3fn_x4
+FP4X4 = mybir.dt.float4_e2m1fn_x4
+ALU = mybir.AluOpType
+ACT = mybir.ActivationFunctionType
+
+P = 128
+PACK = 4
+POOL = 1024
+BANK = 512
+SLOTS = 512
+HALF = SLOTS // 2
+LIST_COLS = SLOTS // 16
+HALF_COLS = LIST_COLS // 2
+
+FLOPS = 2 * 512 * P * 3 * POOL
+
+
+def tile_attend_jury_three_kernel(tc, query, keys_words, keys_scales, notes_words, notes_scales,
+                                   users_words, users_scales, thr, slope,
+                                   offs, offs2, offs3, offs4, offs5, out):
+    nc = tc.nc
+    with ExitStack() as ctx:
+        keep = ctx.enter_context(tc.tile_pool(name="keep", bufs=1))
+        psum = ctx.enter_context(tc.psum_pool(name="psum", bufs=1))
+
+        def list_tile(name):
+            return keep.tile([P, LIST_COLS], U16, name=name)
+
+        def plane_tile(name):
+            plane = keep.tile([P, POOL], U8, name=name, align_bytes=64)
+            nc.vector.memset(plane[:].bitcast(I32), 0)
+            return plane
+
+        def load_scale_rows(queue, plane, scales, r):
+            queue.dma_start(out=plane[r:P:32, :].bitcast(I32), in_=scales[0, r:16:4, :].bitcast(I32))
+
+        keys_plane = plane_tile("keys_plane")
+        notes_plane = plane_tile("notes_plane")
+        users_plane = plane_tile("users_plane")
+        f1 = keep.tile([P, POOL], F32)
+        nc.vector.memset(f1[:], 0.0)
+
+        q_raw = keep.tile([P, PACK, P], F32)
+        keys_sb = keep.tile([P, 2 * POOL], U8, align_bytes=64)
+        notes_sb = keep.tile([P, POOL], U32, align_bytes=64)
+        users_sb = keep.tile([P, 2 * POOL], U8, align_bytes=64)
+        slope_sb = keep.tile([P, 1], F32)
+        thr_sb = keep.tile([P, 1], F32)
+        list1 = list_tile("list1")
+        list2 = list_tile("list2")
+        list3 = list_tile("list3")
+        list4 = list_tile("list4")
+        list5 = list_tile("list5")
+
+        nc.sync.dma_start(out=q_raw[:], in_=query.rearrange("(p j) w -> p j w", j=PACK))
+        for r in range(4):
+            load_scale_rows(nc.sync, keys_plane, keys_scales, r)
+        nc.sync.dma_start(out=keys_sb[:].bitcast(I32), in_=keys_words[0].bitcast(I32))
+        nc.sync.dma_start(out=list1[:], in_=offs)
+        nc.sync.dma_start(out=notes_sb[:].bitcast(I32),
+                          in_=notes_words[0].rearrange("p n t -> p (n t)").bitcast(I32))
+        for r in range(4):
+            load_scale_rows(nc.sync, notes_plane, notes_scales, r)
+        nc.sync.dma_start(out=users_sb[:].bitcast(I32), in_=users_words[0].bitcast(I32))
+        for r in range(2):
+            load_scale_rows(nc.sync, users_plane, users_scales, r)
+        nc.sync.dma_start(out=list2[:], in_=offs2)
+        nc.sync.dma_start(out=list3[:], in_=offs3)
+        nc.sync.dma_start(out=list4[:], in_=offs4)
+        nc.sync.dma_start(out=list5[:], in_=offs5)
+        nc.gpsimd.dma_start(out=slope_sb[:], in_=slope)
+        nc.gpsimd.dma_start(out=thr_sb[:], in_=thr)
+        for r in range(2, 4):
+            load_scale_rows(nc.gpsimd, users_plane, users_scales, r)
+
+        q_grouped = keep.tile([P, P, PACK], BF16, align_bytes=64)
+        nc.vector.tensor_copy(out=q_grouped[:], in_=q_raw[:].rearrange("p j w -> p w j"))
+        q_codes = keep.tile([P, P], U32, align_bytes=64)
+        q_plane = keep.tile([P, P], U8, align_bytes=64)
+        nc.vector.quantize_mx(out=q_codes[:].bitcast(FP8X4), scales=q_plane[:],
+                              in_=q_grouped[:].rearrange("p w j -> p (w j)"))
+
+        def score(name, words, plane, h):
+            bank = psum.tile([P, BANK], F32, name=name)
+            nc.tensor.matmul_mx(out=bank[:], lhsT=q_codes[:].bitcast(FP8X4), lhsT_scale=q_plane[:],
+                                rhs=words, rhs_scale=plane[:, h * BANK:(h + 1) * BANK],
+                                start=True, stop=True)
+            return bank
+
+        def fp4_words(words_sb, h):
+            return words_sb[:, 2 * h * BANK:2 * (h + 1) * BANK].bitcast(FP4X4)
+
+        a_banks = [score("a_bank%d" % h, fp4_words(keys_sb, h), keys_plane, h) for h in range(2)]
+        b_banks = [score("b_bank%d" % h, notes_sb[:, h * BANK:(h + 1) * BANK].bitcast(FP8X4), notes_plane, h)
+                   for h in range(2)]
+        c_banks = [score("c_bank%d" % h, fp4_words(users_sb, h), users_plane, h) for h in range(2)]
+
+        a_sb = keep.tile([P, POOL], F32)
+        b_sb = keep.tile([P, POOL], F32)
+        c_sb = keep.tile([P, POOL], F32)
+        s1 = keep.tile([P, SLOTS], F32)
+        s2 = keep.tile([P, SLOTS], F32)
+        minus_s2 = keep.tile([P, SLOTS], F32)
+        w = keep.tile([P, HALF], F32)
+        cc = keep.tile([P, POOL], F32)
+
+        def slots(h):
+            return slice(h * HALF, (h + 1) * HALF)
+
+        def entries(lst, h):
+            return lst[:, h * HALF_COLS:(h + 1) * HALF_COLS]
+
+        def gate(dst, scores, lst, h):
+            nc.scalar.activation(out=dst[:, slots(h)], in_=scores[:].indirect(entries(lst, h)),
+                                 func=ACT.Sigmoid, bias=thr_sb[:], scale=slope_sb[:])
+
+        def negate_gate(h):
+            nc.scalar.activation(out=minus_s2[:, slots(h)], in_=s2[:, slots(h)], func=ACT.Copy, scale=-1.0)
+
+        def put(h):
+            nc.vector.tensor_tensor(out=f1[:].indirect(entries(list4, h)), in0=w[:],
+                                    in1=minus_s2[:, slots(h)], op=ALU.add)
+
+        nc.vector.tensor_copy(out=a_sb[:, :BANK], in_=a_banks[0][:])
+        nc.vector.tensor_copy(out=a_sb[:, BANK:], in_=a_banks[1][:])
+        gate(s1, a_sb, list1, 0)
+        nc.vector.tensor_copy(out=b_sb[:, :BANK], in_=b_banks[0][:])
+        nc.scalar.copy(out=b_sb[:, BANK:], in_=b_banks[1][:])
+        nc.vector.tensor_copy(out=c_sb[:, :BANK], in_=c_banks[0][:])
+        nc.vector.tensor_copy(out=c_sb[:, BANK:], in_=c_banks[1][:])
+        gate(s2, b_sb, list2, 0)
+        negate_gate(0)
+        nc.vector.tensor_tensor(out=w[:], in0=c_sb[:].indirect(entries(list3, 0)), in1=s1[:, slots(0)], op=ALU.mult)
+        put(0)
+        gate(s1, a_sb, list1, 1)
+        gate(s2, b_sb, list2, 1)
+        negate_gate(1)
+        picked = keep.tile([P, HALF], F32)
+        nc.scalar.activation(out=picked[:], in_=c_sb[:].indirect(entries(list3, 1)), func=ACT.Copy)
+        nc.vector.tensor_tensor(out=w[:], in0=picked[:], in1=s1[:, slots(1)], op=ALU.mult)
+        put(1)
+        nc.vector.tensor_tensor(out=cc[:], in0=c_sb[:], in1=f1[:], op=ALU.add)
+
+        y0 = keep.tile([P, HALF], F32)
+        y1 = keep.tile([P, HALF], F32)
+        nc.vector.tensor_copy(out=y0[:], in_=cc[:].indirect(entries(list5, 0)))
+        nc.scalar.activation(out=y1[:], in_=cc[:].indirect(entries(list5, 1)), func=ACT.Copy)
+        nc.sync.dma_start(out=out[:, slots(0)], in_=y0[:])
+        nc.scalar.dma_start(out=out[:, slots(1)], in_=y1[:])

@@ -47,6 +47,10 @@ def tile_attend_jury_three_kernel(tc, query, keys_words, keys_scales, notes_word
         keys_plane = plane_tile("keys_plane")
         notes_plane = plane_tile("notes_plane")
         users_plane = plane_tile("users_plane")
+        warm_in = keep.tile([P, 1], F32)
+        warm_out = keep.tile([P, 1], F32)
+        nc.vector.memset(warm_in[:], 0.0)
+        nc.scalar.activation(out=warm_out[:], in_=warm_in[:], func=ACT.Sigmoid)
         f1 = keep.tile([P, POOL], F32)
         nc.vector.memset(f1[:], 0.0)
 

@@ -22,6 +22,8 @@ HALF = SLOTS // 2
 LIST_COLS = SLOTS // 16
 HALF_COLS = LIST_COLS // 2
 
+VECTOR_COLS = 752
+
 FLOPS = 2 * 512 * P * 3 * POOL
 
 
@@ -70,25 +72,27 @@ def tile_attend_jury_three_kernel(tc, query, keys_words, keys_scales, notes_word
         for r in range(4):
             load_scale_rows(nc.sync, keys_plane, keys_scales, r)
         nc.sync.dma_start(out=keys_sb[:].bitcast(I32), in_=keys_words[0].bitcast(I32))
-        nc.sync.dma_start(out=list1[:], in_=offs)
+        load_scale_rows(nc.sync, notes_plane, notes_scales, 0)
         nc.sync.dma_start(out=notes_sb[:].bitcast(I32),
                           in_=notes_words[0].rearrange("p n t -> p (n t)").bitcast(I32))
-        for r in range(4):
+        for r in range(1, 4):
             load_scale_rows(nc.sync, notes_plane, notes_scales, r)
+        load_scale_rows(nc.sync, users_plane, users_scales, 0)
         nc.sync.dma_start(out=users_sb[:].bitcast(I32), in_=users_words[0].bitcast(I32))
-        for r in range(2):
+        for r in range(1, 4):
             load_scale_rows(nc.sync, users_plane, users_scales, r)
+        nc.sync.dma_start(out=list1[:], in_=offs)
         nc.sync.dma_start(out=list2[:], in_=offs2)
-        nc.sync.dma_start(out=list3[:], in_=offs3)
         nc.sync.dma_start(out=list4[:], in_=offs4)
+        nc.sync.dma_start(out=list3[:], in_=offs3)
         nc.sync.dma_start(out=list5[:], in_=offs5)
         nc.gpsimd.dma_start(out=slope_sb[:], in_=slope)
         nc.gpsimd.dma_start(out=thr_sb[:], in_=thr)
-        for r in range(2, 4):
-            load_scale_rows(nc.gpsimd, users_plane, users_scales, r)
 
         q_grouped = keep.tile([P, P, PACK], BF16, align_bytes=64)
-        nc.vector.tensor_copy(out=q_grouped[:], in_=q_raw[:].rearrange("p j w -> p w j"))
+        q_view = q_raw[:].rearrange("p j w -> p w j")
+        nc.vector.tensor_copy(out=q_grouped[:, :P // 2, :], in_=q_view[:, :P // 2, :])
+        nc.scalar.copy(out=q_grouped[:, P // 2:, :], in_=q_view[:, P // 2:, :])
         q_codes = keep.tile([P, P], U32, align_bytes=64)
         q_plane = keep.tile([P, P], U8, align_bytes=64)
         nc.vector.quantize_mx(out=q_codes[:].bitcast(FP8X4), scales=q_plane[:],
@@ -112,10 +116,11 @@ def tile_attend_jury_three_kernel(tc, query, keys_words, keys_scales, notes_word
         a_sb = keep.tile([P, POOL], F32)
         b_sb = keep.tile([P, POOL], F32)
         c_sb = keep.tile([P, POOL], F32)
-        s1 = keep.tile([P, SLOTS], F32)
-        s2 = keep.tile([P, SLOTS], F32)
+        stage_a = keep.tile([P, HALF], F32)
+        stage_b = keep.tile([P, HALF], F32)
+        stage_c = keep.tile([P, HALF], F32)
         minus_s2 = keep.tile([P, SLOTS], F32)
-        w = keep.tile([P, HALF], F32)
+        w = keep.tile([P, SLOTS], F32)
         cc = keep.tile([P, POOL], F32)
 
         def slots(h):
@@ -125,35 +130,38 @@ def tile_attend_jury_three_kernel(tc, query, keys_words, keys_scales, notes_word
             return lst[:, h * HALF_COLS:(h + 1) * HALF_COLS]
 
         def gate(dst, scores, lst, h):
-            nc.scalar.activation(out=dst[:, slots(h)], in_=scores[:].indirect(entries(lst, h)),
+            nc.scalar.activation(out=dst, in_=scores[:].indirect(entries(lst, h)),
                                  func=ACT.Sigmoid, bias=thr_sb[:], scale=slope_sb[:])
 
-        def negate_gate(h):
-            nc.scalar.activation(out=minus_s2[:, slots(h)], in_=s2[:, slots(h)], func=ACT.Copy, scale=-1.0)
+        def negate_gate(src, h):
+            nc.scalar.activation(out=minus_s2[:, slots(h)], in_=src[:], func=ACT.Copy, scale=-1.0)
 
         def put(h):
-            nc.vector.tensor_tensor(out=f1[:].indirect(entries(list4, h)), in0=w[:],
+            nc.vector.tensor_tensor(out=f1[:].indirect(entries(list4, h)), in0=w[:, slots(h)],
                                     in1=minus_s2[:, slots(h)], op=ALU.add)
 
-        nc.vector.tensor_copy(out=a_sb[:, :BANK], in_=a_banks[0][:])
+        nc.scalar.copy(out=a_sb[:, :BANK], in_=a_banks[0][:])
         nc.vector.tensor_copy(out=a_sb[:, BANK:], in_=a_banks[1][:])
-        gate(s1, a_sb, list1, 0)
         nc.vector.tensor_copy(out=b_sb[:, :BANK], in_=b_banks[0][:])
         nc.scalar.copy(out=b_sb[:, BANK:], in_=b_banks[1][:])
         nc.vector.tensor_copy(out=c_sb[:, :BANK], in_=c_banks[0][:])
         nc.vector.tensor_copy(out=c_sb[:, BANK:], in_=c_banks[1][:])
-        gate(s2, b_sb, list2, 0)
-        negate_gate(0)
-        nc.vector.tensor_tensor(out=w[:], in0=c_sb[:].indirect(entries(list3, 0)), in1=s1[:, slots(0)], op=ALU.mult)
+        gate(stage_a[:], a_sb, list1, 0)
+        gate(stage_b[:], b_sb, list2, 0)
+        negate_gate(stage_b, 0)
+        nc.vector.tensor_tensor(out=w[:, slots(0)], in0=c_sb[:].indirect(entries(list3, 0)),
+                                in1=stage_a[:], op=ALU.mult)
         put(0)
-        gate(s1, a_sb, list1, 1)
-        gate(s2, b_sb, list2, 1)
-        negate_gate(1)
-        picked = keep.tile([P, HALF], F32)
-        nc.scalar.activation(out=picked[:], in_=c_sb[:].indirect(entries(list3, 1)), func=ACT.Copy)
-        nc.vector.tensor_tensor(out=w[:], in0=picked[:], in1=s1[:, slots(1)], op=ALU.mult)
+        gate(stage_b[:], a_sb, list1, 1)
+        gate(stage_c[:], b_sb, list2, 1)
+        nc.scalar.activation(out=stage_a[:], in_=c_sb[:].indirect(entries(list3, 1)), func=ACT.Copy)
+        negate_gate(stage_c, 1)
+        nc.vector.tensor_tensor(out=w[:, slots(1)], in0=stage_a[:], in1=stage_b[:], op=ALU.mult)
         put(1)
-        nc.vector.tensor_tensor(out=cc[:], in0=c_sb[:], in1=f1[:], op=ALU.add)
+        nc.gpsimd.tensor_tensor(out=cc[:, VECTOR_COLS:], in0=c_sb[:, VECTOR_COLS:], in1=f1[:, VECTOR_COLS:], op=ALU.add)
+        nc.vector.tensor_tensor(out=cc[:, :BANK], in0=c_banks[0][:], in1=f1[:, :BANK], op=ALU.add)
+        nc.vector.tensor_tensor(out=cc[:, BANK:VECTOR_COLS], in0=c_banks[1][:, :VECTOR_COLS - BANK],
+                                in1=f1[:, BANK:VECTOR_COLS], op=ALU.add)
 
         y0 = keep.tile([P, HALF], F32)
         y1 = keep.tile([P, HALF], F32)

@@ -52,9 +52,9 @@ def tile_attend_jury_three_kernel(tc, query, keys_words, keys_scales, notes_word
         warm_in = keep.tile([P, 1], F32)
         warm_out = keep.tile([P, 1], F32)
         nc.vector.memset(warm_in[:], 0.0)
-        nc.scalar.activation(out=warm_out[:], in_=warm_in[:], func=ACT.Sigmoid)
         f1 = keep.tile([P, POOL], F32)
-        nc.vector.memset(f1[:], 0.0)
+        nc.vector.memset(f1[:, :BANK - 1], 0.0)
+        nc.vector.memset(f1[:, BANK - 1:], 0.0)
 
         q_raw = keep.tile([P, PACK, P], F32)
         keys_sb = keep.tile([P, 2 * POOL], U8, align_bytes=64)
@@ -69,9 +69,12 @@ def tile_attend_jury_three_kernel(tc, query, keys_words, keys_scales, notes_word
         list5 = list_tile("list5")
 
         nc.sync.dma_start(out=q_raw[:], in_=query.rearrange("(p j) w -> p j w", j=PACK))
-        for r in range(4):
-            load_scale_rows(nc.sync, keys_plane, keys_scales, r)
+        for r in range(2):
+            load_scale_rows(nc.scalar, keys_plane, keys_scales, r)
+        nc.scalar.activation(out=warm_out[:], in_=warm_in[:], func=ACT.Sigmoid)
+        load_scale_rows(nc.sync, keys_plane, keys_scales, 2)
         nc.sync.dma_start(out=keys_sb[:].bitcast(I32), in_=keys_words[0].bitcast(I32))
+        load_scale_rows(nc.sync, keys_plane, keys_scales, 3)
         load_scale_rows(nc.sync, notes_plane, notes_scales, 0)
         nc.sync.dma_start(out=notes_sb[:].bitcast(I32),
                           in_=notes_words[0].rearrange("p n t -> p (n t)").bitcast(I32))
@@ -79,20 +82,19 @@ def tile_attend_jury_three_kernel(tc, query, keys_words, keys_scales, notes_word
             load_scale_rows(nc.sync, notes_plane, notes_scales, r)
         load_scale_rows(nc.sync, users_plane, users_scales, 0)
         nc.sync.dma_start(out=users_sb[:].bitcast(I32), in_=users_words[0].bitcast(I32))
-        for r in range(1, 4):
+        for r in range(1, 3):
             load_scale_rows(nc.sync, users_plane, users_scales, r)
         nc.sync.dma_start(out=list1[:], in_=offs)
         nc.sync.dma_start(out=list2[:], in_=offs2)
-        nc.sync.dma_start(out=list4[:], in_=offs4)
         nc.sync.dma_start(out=list3[:], in_=offs3)
+        nc.sync.dma_start(out=list4[:], in_=offs4)
         nc.sync.dma_start(out=list5[:], in_=offs5)
         nc.gpsimd.dma_start(out=slope_sb[:], in_=slope)
         nc.gpsimd.dma_start(out=thr_sb[:], in_=thr)
+        load_scale_rows(nc.gpsimd, users_plane, users_scales, 3)
 
         q_grouped = keep.tile([P, P, PACK], BF16, align_bytes=64)
-        q_view = q_raw[:].rearrange("p j w -> p w j")
-        nc.vector.tensor_copy(out=q_grouped[:, :P // 2, :], in_=q_view[:, :P // 2, :])
-        nc.scalar.copy(out=q_grouped[:, P // 2:, :], in_=q_view[:, P // 2:, :])
+        nc.vector.tensor_copy(out=q_grouped[:], in_=q_raw[:].rearrange("p j w -> p w j"))
         q_codes = keep.tile([P, P], U32, align_bytes=64)
         q_plane = keep.tile([P, P], U8, align_bytes=64)
         nc.vector.quantize_mx(out=q_codes[:].bitcast(FP8X4), scales=q_plane[:],
@@ -116,9 +118,8 @@ def tile_attend_jury_three_kernel(tc, query, keys_words, keys_scales, notes_word
         a_sb = keep.tile([P, POOL], F32)
         b_sb = keep.tile([P, POOL], F32)
         c_sb = keep.tile([P, POOL], F32)
-        stage_a = keep.tile([P, HALF], F32)
-        stage_b = keep.tile([P, HALF], F32)
-        stage_c = keep.tile([P, HALF], F32)
+        s1 = keep.tile([P, SLOTS], F32)
+        s2_half = keep.tile([P, HALF], F32)
         minus_s2 = keep.tile([P, SLOTS], F32)
         w = keep.tile([P, SLOTS], F32)
         cc = keep.tile([P, POOL], F32)
@@ -133,8 +134,9 @@ def tile_attend_jury_three_kernel(tc, query, keys_words, keys_scales, notes_word
             nc.scalar.activation(out=dst, in_=scores[:].indirect(entries(lst, h)),
                                  func=ACT.Sigmoid, bias=thr_sb[:], scale=slope_sb[:])
 
-        def negate_gate(src, h):
-            nc.scalar.activation(out=minus_s2[:, slots(h)], in_=src[:], func=ACT.Copy, scale=-1.0)
+        def negated_note_gate(h):
+            gate(s2_half[:], b_sb, list2, h)
+            nc.scalar.activation(out=minus_s2[:, slots(h)], in_=s2_half[:], func=ACT.Copy, scale=-1.0)
 
         def put(h):
             nc.vector.tensor_tensor(out=f1[:].indirect(entries(list4, h)), in0=w[:, slots(h)],
@@ -142,21 +144,20 @@ def tile_attend_jury_three_kernel(tc, query, keys_words, keys_scales, notes_word
 
         nc.scalar.copy(out=a_sb[:, :BANK], in_=a_banks[0][:])
         nc.vector.tensor_copy(out=a_sb[:, BANK:], in_=a_banks[1][:])
-        nc.vector.tensor_copy(out=b_sb[:, :BANK], in_=b_banks[0][:])
-        nc.scalar.copy(out=b_sb[:, BANK:], in_=b_banks[1][:])
-        nc.vector.tensor_copy(out=c_sb[:, :BANK], in_=c_banks[0][:])
-        nc.vector.tensor_copy(out=c_sb[:, BANK:], in_=c_banks[1][:])
-        gate(stage_a[:], a_sb, list1, 0)
-        gate(stage_b[:], b_sb, list2, 0)
-        negate_gate(stage_b, 0)
+        for h in range(2):
+            nc.vector.tensor_copy(out=b_sb[:, h * BANK:(h + 1) * BANK], in_=b_banks[h][:])
+        for h in range(2):
+            nc.vector.tensor_copy(out=c_sb[:, h * BANK:(h + 1) * BANK], in_=c_banks[h][:])
+        for h in range(2):
+            gate(s1[:, slots(h)], a_sb, list1, h)
+        negated_note_gate(0)
+        picked = keep.tile([P, HALF], F32)
+        nc.scalar.activation(out=picked[:], in_=c_sb[:].indirect(entries(list3, 1)), func=ACT.Copy)
         nc.vector.tensor_tensor(out=w[:, slots(0)], in0=c_sb[:].indirect(entries(list3, 0)),
-                                in1=stage_a[:], op=ALU.mult)
+                                in1=s1[:, slots(0)], op=ALU.mult)
+        nc.vector.tensor_tensor(out=w[:, slots(1)], in0=picked[:], in1=s1[:, slots(1)], op=ALU.mult)
         put(0)
-        gate(stage_b[:], a_sb, list1, 1)
-        gate(stage_c[:], b_sb, list2, 1)
-        nc.scalar.activation(out=stage_a[:], in_=c_sb[:].indirect(entries(list3, 1)), func=ACT.Copy)
-        negate_gate(stage_c, 1)
-        nc.vector.tensor_tensor(out=w[:, slots(1)], in0=stage_a[:], in1=stage_b[:], op=ALU.mult)
+        negated_note_gate(1)
         put(1)
         nc.gpsimd.tensor_tensor(out=cc[:, VECTOR_COLS:], in0=c_sb[:, VECTOR_COLS:], in1=f1[:, VECTOR_COLS:], op=ALU.add)
         nc.vector.tensor_tensor(out=cc[:, :BANK], in0=c_banks[0][:], in1=f1[:, :BANK], op=ALU.add)

@@ -53,8 +53,7 @@ def tile_attend_jury_three_kernel(tc, query, keys_words, keys_scales, notes_word
         warm_out = keep.tile([P, 1], F32)
         nc.vector.memset(warm_in[:], 0.0)
         f1 = keep.tile([P, POOL], F32)
-        nc.vector.memset(f1[:, :BANK - 1], 0.0)
-        nc.vector.memset(f1[:, BANK - 1:], 0.0)
+        nc.vector.memset(f1[:], 0.0)
 
         q_raw = keep.tile([P, PACK, P], F32)
         keys_sb = keep.tile([P, 2 * POOL], U8, align_bytes=64)
@@ -82,16 +81,15 @@ def tile_attend_jury_three_kernel(tc, query, keys_words, keys_scales, notes_word
             load_scale_rows(nc.sync, notes_plane, notes_scales, r)
         load_scale_rows(nc.sync, users_plane, users_scales, 0)
         nc.sync.dma_start(out=users_sb[:].bitcast(I32), in_=users_words[0].bitcast(I32))
-        for r in range(1, 3):
+        for r in range(1, 4):
             load_scale_rows(nc.sync, users_plane, users_scales, r)
         nc.sync.dma_start(out=list1[:], in_=offs)
         nc.sync.dma_start(out=list2[:], in_=offs2)
-        nc.sync.dma_start(out=list3[:], in_=offs3)
         nc.sync.dma_start(out=list4[:], in_=offs4)
+        nc.sync.dma_start(out=list3[:], in_=offs3)
         nc.sync.dma_start(out=list5[:], in_=offs5)
         nc.gpsimd.dma_start(out=slope_sb[:], in_=slope)
         nc.gpsimd.dma_start(out=thr_sb[:], in_=thr)
-        load_scale_rows(nc.gpsimd, users_plane, users_scales, 3)
 
         q_grouped = keep.tile([P, P, PACK], BF16, align_bytes=64)
         nc.vector.tensor_copy(out=q_grouped[:], in_=q_raw[:].rearrange("p j w -> p w j"))
@@ -118,8 +116,9 @@ def tile_attend_jury_three_kernel(tc, query, keys_words, keys_scales, notes_word
         a_sb = keep.tile([P, POOL], F32)
         b_sb = keep.tile([P, POOL], F32)
         c_sb = keep.tile([P, POOL], F32)
-        s1 = keep.tile([P, SLOTS], F32)
-        s2_half = keep.tile([P, HALF], F32)
+        stage_a = keep.tile([P, HALF], F32)
+        stage_b = keep.tile([P, HALF], F32)
+        stage_c = keep.tile([P, HALF], F32)
         minus_s2 = keep.tile([P, SLOTS], F32)
         w = keep.tile([P, SLOTS], F32)
         cc = keep.tile([P, POOL], F32)
@@ -134,9 +133,8 @@ def tile_attend_jury_three_kernel(tc, query, keys_words, keys_scales, notes_word
             nc.scalar.activation(out=dst, in_=scores[:].indirect(entries(lst, h)),
                                  func=ACT.Sigmoid, bias=thr_sb[:], scale=slope_sb[:])
 
-        def negated_note_gate(h):
-            gate(s2_half[:], b_sb, list2, h)
-            nc.scalar.activation(out=minus_s2[:, slots(h)], in_=s2_half[:], func=ACT.Copy, scale=-1.0)
+        def negate_gate(src, h):
+            nc.scalar.activation(out=minus_s2[:, slots(h)], in_=src[:], func=ACT.Copy, scale=-1.0)
 
         def put(h):
             nc.vector.tensor_tensor(out=f1[:].indirect(entries(list4, h)), in0=w[:, slots(h)],
@@ -144,20 +142,21 @@ def tile_attend_jury_three_kernel(tc, query, keys_words, keys_scales, notes_word
 
         nc.scalar.copy(out=a_sb[:, :BANK], in_=a_banks[0][:])
         nc.vector.tensor_copy(out=a_sb[:, BANK:], in_=a_banks[1][:])
-        for h in range(2):
-            nc.vector.tensor_copy(out=b_sb[:, h * BANK:(h + 1) * BANK], in_=b_banks[h][:])
-        for h in range(2):
-            nc.vector.tensor_copy(out=c_sb[:, h * BANK:(h + 1) * BANK], in_=c_banks[h][:])
-        for h in range(2):
-            gate(s1[:, slots(h)], a_sb, list1, h)
-        negated_note_gate(0)
-        picked = keep.tile([P, HALF], F32)
-        nc.scalar.activation(out=picked[:], in_=c_sb[:].indirect(entries(list3, 1)), func=ACT.Copy)
+        nc.vector.tensor_copy(out=b_sb[:, :BANK], in_=b_banks[0][:])
+        nc.scalar.copy(out=b_sb[:, BANK:], in_=b_banks[1][:])
+        nc.vector.tensor_copy(out=c_sb[:, :BANK], in_=c_banks[0][:])
+        nc.vector.tensor_copy(out=c_sb[:, BANK:], in_=c_banks[1][:])
+        gate(stage_a[:], a_sb, list1, 0)
+        gate(stage_b[:], b_sb, list2, 0)
+        negate_gate(stage_b, 0)
         nc.vector.tensor_tensor(out=w[:, slots(0)], in0=c_sb[:].indirect(entries(list3, 0)),
-                                in1=s1[:, slots(0)], op=ALU.mult)
-        nc.vector.tensor_tensor(out=w[:, slots(1)], in0=picked[:], in1=s1[:, slots(1)], op=ALU.mult)
+                                in1=stage_a[:], op=ALU.mult)
         put(0)
-        negated_note_gate(1)
+        gate(stage_b[:], a_sb, list1, 1)
+        gate(stage_c[:], b_sb, list2, 1)
+        nc.scalar.activation(out=stage_a[:], in_=c_sb[:].indirect(entries(list3, 1)), func=ACT.Copy)
+        negate_gate(stage_c, 1)
+        nc.vector.tensor_tensor(out=w[:, slots(1)], in0=stage_a[:], in1=stage_b[:], op=ALU.mult)
         put(1)
         nc.gpsimd.tensor_tensor(out=cc[:, VECTOR_COLS:], in0=c_sb[:, VECTOR_COLS:], in1=f1[:, VECTOR_COLS:], op=ALU.add)
         nc.vector.tensor_tensor(out=cc[:, :BANK], in0=c_banks[0][:], in1=f1[:, :BANK], op=ALU.add)

from contextlib import ExitStack

import concourse.mybir as mybir

F32 = mybir.dt.float32
BF16 = mybir.dt.bfloat16
I32 = mybir.dt.int32
U32 = mybir.dt.uint32
U16 = mybir.dt.uint16
U8 = mybir.dt.uint8
FP8X4 = mybir.dt.float8_e4m3fn_x4
FP4X4 = mybir.dt.float4_e2m1fn_x4
ALU = mybir.AluOpType
ACT = mybir.ActivationFunctionType

P = 128
PACK = 4
POOL = 1024
BANK = 512
SLOTS = 512
HALF = SLOTS // 2
LIST_COLS = SLOTS // 16
HALF_COLS = LIST_COLS // 2

VECTOR_COLS = 752

FLOPS = 2 * 512 * P * 3 * POOL


def tile_attend_jury_three_kernel(tc, query, keys_words, keys_scales, notes_words, notes_scales,
                                   users_words, users_scales, thr, slope,
                                   offs, offs2, offs3, offs4, offs5, out):
    nc = tc.nc
    with ExitStack() as ctx:
        keep = ctx.enter_context(tc.tile_pool(name="keep", bufs=1))
        psum = ctx.enter_context(tc.psum_pool(name="psum", bufs=1))

        def list_tile(name):
            return keep.tile([P, LIST_COLS], U16, name=name)

        def plane_tile(name):
            plane = keep.tile([P, POOL], U8, name=name, align_bytes=64)
            nc.vector.memset(plane[:].bitcast(I32), 0)
            return plane

        def load_scale_rows(queue, plane, scales, r):
            queue.dma_start(out=plane[r:P:32, :].bitcast(I32), in_=scales[0, r:16:4, :].bitcast(I32))

        keys_plane = plane_tile("keys_plane")
        notes_plane = plane_tile("notes_plane")
        users_plane = plane_tile("users_plane")
        warm_in = keep.tile([P, 1], F32)
        warm_out = keep.tile([P, 1], F32)
        nc.vector.memset(warm_in[:], 0.0)
        f1 = keep.tile([P, POOL], F32)
        nc.vector.memset(f1[:], 0.0)

        q_raw = keep.tile([P, PACK, P], F32)
        keys_sb = keep.tile([P, 2 * POOL], U8, align_bytes=64)
        notes_sb = keep.tile([P, POOL], U32, align_bytes=64)
        users_sb = keep.tile([P, 2 * POOL], U8, align_bytes=64)
        slope_sb = keep.tile([P, 1], F32)
        thr_sb = keep.tile([P, 1], F32)
        list1 = list_tile("list1")
        list2 = list_tile("list2")
        list3 = list_tile("list3")
        list4 = list_tile("list4")
        list5 = list_tile("list5")

        nc.sync.dma_start(out=q_raw[:], in_=query.rearrange("(p j) w -> p j w", j=PACK))
        for r in range(2):
            load_scale_rows(nc.scalar, keys_plane, keys_scales, r)
        nc.scalar.activation(out=warm_out[:], in_=warm_in[:], func=ACT.Sigmoid)
        load_scale_rows(nc.sync, keys_plane, keys_scales, 2)
        nc.sync.dma_start(out=keys_sb[:].bitcast(I32), in_=keys_words[0].bitcast(I32))
        load_scale_rows(nc.sync, keys_plane, keys_scales, 3)
        load_scale_rows(nc.sync, notes_plane, notes_scales, 0)
        nc.sync.dma_start(out=notes_sb[:].bitcast(I32),
                          in_=notes_words[0].rearrange("p n t -> p (n t)").bitcast(I32))
        for r in range(1, 4):
            load_scale_rows(nc.sync, notes_plane, notes_scales, r)
        load_scale_rows(nc.sync, users_plane, users_scales, 0)
        nc.sync.dma_start(out=users_sb[:].bitcast(I32), in_=users_words[0].bitcast(I32))
        for r in range(1, 4):
            load_scale_rows(nc.sync, users_plane, users_scales, r)
        nc.sync.dma_start(out=list1[:], in_=offs)
        nc.sync.dma_start(out=list2[:], in_=offs2)
        nc.sync.dma_start(out=list4[:], in_=offs4)
        nc.sync.dma_start(out=list3[:], in_=offs3)
        nc.sync.dma_start(out=list5[:], in_=offs5)
        nc.gpsimd.dma_start(out=slope_sb[:], in_=slope)
        nc.gpsimd.dma_start(out=thr_sb[:], in_=thr)

        q_grouped = keep.tile([P, P, PACK], BF16, align_bytes=64)
        nc.vector.tensor_copy(out=q_grouped[:], in_=q_raw[:].rearrange("p j w -> p w j"))
        q_codes = keep.tile([P, P], U32, align_bytes=64)
        q_plane = keep.tile([P, P], U8, align_bytes=64)
        nc.vector.quantize_mx(out=q_codes[:].bitcast(FP8X4), scales=q_plane[:],
                              in_=q_grouped[:].rearrange("p w j -> p (w j)"))

        def score(name, words, plane, h):
            bank = psum.tile([P, BANK], F32, name=name)
            nc.tensor.matmul_mx(out=bank[:], lhsT=q_codes[:].bitcast(FP8X4), lhsT_scale=q_plane[:],
                                rhs=words, rhs_scale=plane[:, h * BANK:(h + 1) * BANK],
                                start=True, stop=True)
            return bank

        def fp4_words(words_sb, h):
            return words_sb[:, 2 * h * BANK:2 * (h + 1) * BANK].bitcast(FP4X4)

        a_banks = [score("a_bank%d" % h, fp4_words(keys_sb, h), keys_plane, h) for h in range(2)]
        b_banks = [score("b_bank%d" % h, notes_sb[:, h * BANK:(h + 1) * BANK].bitcast(FP8X4), notes_plane, h)
                   for h in range(2)]
        c_banks = [score("c_bank%d" % h, fp4_words(users_sb, h), users_plane, h) for h in range(2)]

        a_sb = keep.tile([P, POOL], F32)
        b_sb = keep.tile([P, POOL], F32)
        c_sb = keep.tile([P, POOL], F32)
        stage_a = keep.tile([P, HALF], F32)
        stage_b = keep.tile([P, HALF], F32)
        stage_c = keep.tile([P, HALF], F32)
        minus_s2 = keep.tile([P, SLOTS], F32)
        w = keep.tile([P, SLOTS], F32)
        cc = keep.tile([P, POOL], F32)

        def slots(h):
            return slice(h * HALF, (h + 1) * HALF)

        def entries(lst, h):
            return lst[:, h * HALF_COLS:(h + 1) * HALF_COLS]

        def gate(dst, scores, lst, h):
            nc.scalar.activation(out=dst, in_=scores[:].indirect(entries(lst, h)),
                                 func=ACT.Sigmoid, bias=thr_sb[:], scale=slope_sb[:])

        def negate_gate(src, h):
            nc.scalar.activation(out=minus_s2[:, slots(h)], in_=src[:], func=ACT.Copy, scale=-1.0)

        def put(h):
            nc.vector.tensor_tensor(out=f1[:].indirect(entries(list4, h)), in0=w[:, slots(h)],
                                    in1=minus_s2[:, slots(h)], op=ALU.add)

        nc.scalar.copy(out=a_sb[:, :BANK], in_=a_banks[0][:])
        nc.vector.tensor_copy(out=a_sb[:, BANK:], in_=a_banks[1][:])
        nc.vector.tensor_copy(out=b_sb[:, :BANK], in_=b_banks[0][:])
        nc.scalar.copy(out=b_sb[:, BANK:], in_=b_banks[1][:])
        nc.vector.tensor_copy(out=c_sb[:, :BANK], in_=c_banks[0][:])
        nc.vector.tensor_copy(out=c_sb[:, BANK:], in_=c_banks[1][:])
        gate(stage_a[:], a_sb, list1, 0)
        gate(stage_b[:], b_sb, list2, 0)
        negate_gate(stage_b, 0)
        nc.vector.tensor_tensor(out=w[:, slots(0)], in0=c_sb[:].indirect(entries(list3, 0)),
                                in1=stage_a[:], op=ALU.mult)
        put(0)
        gate(stage_b[:], a_sb, list1, 1)
        gate(stage_c[:], b_sb, list2, 1)
        nc.scalar.activation(out=stage_a[:], in_=c_sb[:].indirect(entries(list3, 1)), func=ACT.Copy)
        negate_gate(stage_c, 1)
        nc.vector.tensor_tensor(out=w[:, slots(1)], in0=stage_a[:], in1=stage_b[:], op=ALU.mult)
        put(1)
        nc.gpsimd.tensor_tensor(out=cc[:, VECTOR_COLS:], in0=c_sb[:, VECTOR_COLS:], in1=f1[:, VECTOR_COLS:], op=ALU.add)
        nc.vector.tensor_tensor(out=cc[:, :BANK], in0=c_banks[0][:], in1=f1[:, :BANK], op=ALU.add)
        nc.vector.tensor_tensor(out=cc[:, BANK:VECTOR_COLS], in0=c_banks[1][:, :VECTOR_COLS - BANK],
                                in1=f1[:, BANK:VECTOR_COLS], op=ALU.add)

        y0 = keep.tile([P, HALF], F32)
        y1 = keep.tile([P, HALF], F32)
        nc.vector.tensor_copy(out=y0[:], in_=cc[:].indirect(entries(list5, 0)))
        nc.scalar.activation(out=y1[:], in_=cc[:].indirect(entries(list5, 1)), func=ACT.Copy)
        nc.sync.dma_start(out=out[:, slots(0)], in_=y0[:])
        nc.scalar.dma_start(out=out[:, slots(1)], in_=y1[:])
